import numpy as np
import ml_dtypes


def mxq(x, axis, fmt="e4m3"):
    dtype, down = {"e4m3": (ml_dtypes.float8_e4m3fn, 7), "e5m2": (ml_dtypes.float8_e5m2, 14)}[fmt]
    v = np.moveaxis(np.asarray(x, np.float32).astype(ml_dtypes.bfloat16).astype(np.float64), axis, -1)
    blocks = v.reshape(v.shape[:-1] + (-1, 32))
    amax = np.abs(blocks).max(-1, keepdims=True)
    byte = np.maximum(np.where(amax > 0, np.frexp(amax)[1] - 1 + 127, 0) - down, 1)
    scale = np.exp2(byte - 127.0)
    codes = (blocks / scale).astype(np.float32).astype(dtype).astype(np.float64)
    return np.moveaxis((codes * scale).reshape(v.shape), -1, axis)


WIDE = False


def mx_kscale(k):
    if not WIDE:
        return np.ones(k)
    levels = np.array([10, -10, 5, -5, 0])
    if k % 512:
        return np.exp2(np.random.permutation(np.resize(levels, k // 32))).repeat(32)
    a = np.empty((k // 512, 16))
    for p in range(k // 512):
        a[p, :8] = np.random.permutation(np.resize(levels, 8))
        for g in range(8):
            far = levels[np.abs(levels - a[p, g]) >= 10]
            a[p, g + 8] = far[np.random.randint(len(far))]
    return np.exp2(a.ravel()).repeat(32)


def f64(x):
    return np.asarray(x).astype(np.float64)


def striped(idx):
    return np.tile(np.asarray(idx).reshape(-1, 16).T, (8, 1)).astype(np.uint16)


def unstriped(offs):
    return offs[:16].T.reshape(-1).astype(np.int64)


E2M1 = np.array([0.0, 0.5, 1.0, 1.5, 2.0, 3.0, 4.0, 6.0, -0.0, -0.5, -1.0, -1.5, -2.0, -3.0, -4.0, -6.0])


def pack_weight(w, fmt):
    k, n = w.shape
    w = f64(np.asarray(w, np.float32).astype(ml_dtypes.bfloat16)).reshape(k // 32, 32, n)
    amax = np.abs(w).max(1)
    if fmt == "e4m3":
        byte = np.frexp(amax)[1] - 1 + 127 - 7
    else:
        mant, ex = np.frexp(amax / 6.0)
        byte = np.where(mant > 0.5, ex, ex - 1) + 127
    byte = np.clip(np.where(amax > 0, byte, 1), 1, 254)
    scaled = (w * np.exp2(127.0 - byte)[:, None, :]).reshape(k, n).astype(np.float32)
    by_word = np.ascontiguousarray(scaled.reshape(k // 512, 128, 4, n).transpose(0, 1, 3, 2))
    if fmt == "e4m3":
        words = by_word.astype(ml_dtypes.float8_e4m3fn).view(np.uint8)
    else:
        c = by_word.astype(ml_dtypes.float4_e2m1fn).view(np.uint8) & 0xF
        words = (c[..., 0::2] | (c[..., 1::2] << 4)).reshape(k // 512, 128, 2 * n)
    return np.ascontiguousarray(words), np.ascontiguousarray(byte.astype(np.uint8).reshape(k // 512, 16, n))


def unpack_weight(words, scales, fmt):
    g, _, n = scales.shape
    words = np.ascontiguousarray(words).reshape(g, 128, n, -1)
    if fmt == "e4m3":
        vals = words.view(ml_dtypes.float8_e4m3fn).astype(np.float64)
    else:
        nib = np.empty((g, 128, n, 4), np.uint8)
        nib[..., 0::2] = words & 0xF
        nib[..., 1::2] = words >> 4
        vals = E2M1[nib]
    vals = vals * np.repeat(np.exp2(scales.astype(np.float64) - 127.0), 8, axis=1)[..., None]
    return vals.transpose(0, 1, 3, 2).reshape(g * 512, n)


def bf(x):
    return np.asarray(x, np.float32).astype(ml_dtypes.bfloat16)


def planes(Y):
    r, m = Y.shape
    b = f64(bf(Y)).reshape(r // 32, 32, m)
    amax = np.abs(b).max(1)
    byte = np.clip(np.where(amax > 0, np.frexp(amax)[1] - 1 + 127 - 7, 1), 1, 254)
    codes = (b * np.exp2(127.0 - byte)[:, None, :]).reshape(r, m).astype(np.float32).astype(ml_dtypes.float8_e4m3fn).view(np.uint8)
    words = codes.reshape(r // 512, 128, 4, m).transpose(0, 1, 3, 2)
    return np.ascontiguousarray(words), np.ascontiguousarray(byte.astype(np.uint8).reshape(r // 512, 16, m))


D, T, I, Q, E, G, M = 512, 2048, 512, 256, 512, 64, 1024


def setup_inputs():
    n = np.random.standard_normal
    idx = np.random.permutation(T)[:I]
    idx2 = np.random.permutation(T)[:I]
    idx3 = np.random.permutation(M)[:Q]
    fd = mx_kscale(D)
    fi = mx_kscale(I)
    ti = np.ones(T)
    ti[idx] = fi
    keysp = pack_weight(n((D, T)) / fd[:, None], "e2m1")
    return {
        "query": (n((D, Q)) * 1.0 / np.sqrt(D) * fd[:, None]).astype(np.float32),
        "query2": (n((D, Q)) * 1.0 / np.sqrt(D) * fd[:, None]).astype(np.float32),
        "keys_words": keysp[0],
        "keys_scales": keysp[1],
        "lam": (np.random.uniform(1.0, 3.0, (Q, 1))).astype(np.float32),
        "os": (np.random.uniform(4.0, 16.0, (1, I)) * fi).astype(np.float32),
        "vals": (n((E, T)) / ti).astype(np.float32),
        "member": (n((E, M))).astype(np.float32),
        "mgain": np.tile(np.random.uniform(0.5, 2.0, M), (128, 1)).astype(np.float32),
        "offs": striped(idx),
        "offs2": striped(idx2),
        "offs3": striped(idx3),
    }


def reference(query, query2, keys_words, keys_scales, lam, os, vals, member, mgain, offs, offs2, offs3):
    idx = unstriped(offs)
    idx2 = unstriped(offs2)
    idx3 = unstriped(offs3)
    keysu = unpack_weight(keys_words, keys_scales, "e2m1")
    queryq = mxq(f64(query), 0, "e4m3")
    a = queryq.T @ keysu
    query2q = mxq(f64(query2), 0, "e4m3")
    b = query2q.T @ keysu
    la = np.square(a[:, idx]) + np.square(b[:, idx])
    lb = np.square(a[:, idx2]) + np.square(b[:, idx2])
    s = (a[:, idx] * a[:, idx2] + b[:, idx] * b[:, idx2]) / np.sqrt(la * lb + 0.5) * f64(lam)
    p = np.exp(s)
    pg = p.reshape(Q, G, I // G).sum(axis=2)
    z0 = np.sum(pg, axis=1, keepdims=True)
    k0 = 1.0 / (z0 - pg)
    kr = np.repeat(k0, I // G, axis=1)
    w = p * kr
    wo1 = w * f64(os)
    wt1 = wo1.T
    vt1 = f64(vals)[:, idx].T
    vt1q = mxq(vt1, 0, "e4m3")
    wt1q = mxq(wt1, 0, "e4m3")
    o = vt1q.T @ wt1q
    y = o * f64(mgain)[:1][:, idx3] + f64(member)[:, idx3]
    words, scales = planes(y)
    return y, words, scales

@@ -1,0 +1,279 @@
+from contextlib import ExitStack
+
+import concourse.mybir as mybir
+from concourse.masks import make_identity
+
+D, T, I, Q, E, G, M = 512, 2048, 512, 256, 512, 64, 1024
+FLOPS = 2 * (2 * D * Q * T) + 2 * I * E * Q
+
+F32 = mybir.dt.float32
+BF16 = mybir.dt.bfloat16
+I32 = mybir.dt.int32
+U32 = mybir.dt.uint32
+U16 = mybir.dt.uint16
+U8 = mybir.dt.uint8
+FP8X4 = mybir.dt.float8_e4m3fn_x4
+FP4X4 = mybir.dt.float4_e2m1fn_x4
+ALU = mybir.AluOpType
+ACT = mybir.ActivationFunctionType
+AXIS = mybir.AxisListType
+
+P = 128
+PACK = 4
+BANK = 512
+RUN = I // G
+Q_TILES = Q // P
+
+
+def tile_attend_planecos_outside_bymember_pl_kernel(
+    tc, query, query2, keys_words, keys_scales, lam, slot_factor, vals, member, mgain, offs, offs2, offs3, out_0, out_1, out_2
+):
+    nc = tc.nc
+    with ExitStack() as ctx:
+        keep = ctx.enter_context(tc.tile_pool(name="keep", bufs=1))
+        psum = ctx.enter_context(tc.psum_pool(name="psum", bufs=1))
+
+        def sbuf(name, shape, dtype, tag=None):
+            return keep.tile(shape, dtype, name=name, tag=tag or name, align_bytes=64)
+
+        def bank(name, shape, tag, bufs):
+            return psum.tile(shape, F32, name=name, tag=tag, bufs=bufs)
+
+        q_raw = [sbuf(f"q_raw{n}", [P, PACK, Q], F32) for n in range(2)]
+        k_words = [sbuf(f"k_words{n}", [P, T], U8) for n in range(2)]
+        k_scales = sbuf("k_scales", [P, T], U8)
+        list1 = keep.tile([P, I // 16], U16, name="list1")
+        list2 = keep.tile([P, I // 16], U16, name="list2")
+        list3 = keep.tile([P, Q // 16], U16, name="list3")
+        lam_col = sbuf("lam_col", [P, Q_TILES], F32)
+        os_col = sbuf("os_col", [P, PACK], F32)
+        val_rows = [sbuf(f"val_rows{j}", [P, T], F32) for j in range(PACK)]
+        mem_rows = [sbuf(f"mem_rows{j}", [P, M], F32) for j in range(PACK)]
+        gain_rows = sbuf("gain_rows", [P, M], F32)
+
+        nc.sync.dma_start(q_raw[0][:], query.rearrange("(p j) q -> p j q", j=PACK))
+        nc.sync.dma_start(k_words[0][:].bitcast(I32), keys_words[0, :, :T].bitcast(I32))
+        for quad in range(4):
+            nc.sync.dma_start(
+                k_scales[32 * quad : 32 * quad + 4, :].bitcast(I32), keys_scales[0, 4 * quad : 4 * quad + 4, :].bitcast(I32)
+            )
+        nc.sync.dma_start(k_words[1][:].bitcast(I32), keys_words[0, :, T:].bitcast(I32))
+        nc.sync.dma_start(q_raw[1][:], query2.rearrange("(p j) q -> p j q", j=PACK))
+        nc.sync.dma_start(list1[:], offs)
+        nc.sync.dma_start(list2[:], offs2)
+        vals_dealt = vals.rearrange("(p j) t -> p j t", j=PACK)
+        for j in range(PACK):
+            nc.sync.dma_start(val_rows[j][:], vals_dealt[:, j, :])
+        with nc.allow_non_contiguous_dma(reason="one score factor a partition"):
+            nc.sync.dma_start(lam_col[:], lam.rearrange("(h p) o -> p (h o)", p=P))
+        nc.sync.dma_start(os_col[:], slot_factor.rearrange("o (p t) -> p (o t)", t=PACK))
+        nc.sync.dma_start(list3[:], offs3)
+        nc.sync.dma_start(gain_rows[:], mgain)
+        member_dealt = member.rearrange("(p j) m -> p j m", j=PACK)
+        for j in range(PACK):
+            nc.sync.dma_start(mem_rows[j][:], member_dealt[:, j, :])
+
+        ident = sbuf("ident", [P, P], F32)
+        make_identity(nc, ident[:])
+
+        q_words, q_scales = [], []
+        for n in range(2):
+            grouped = sbuf(f"q_grouped{n}", [P, Q, PACK], BF16)
+            dst = grouped[:].rearrange("p (c i) t -> p c t i", i=4)
+            src = q_raw[n][:].rearrange("p t (c i) -> p c t i", i=4)
+            nc.vector.tensor_copy(dst, src)
+            words = sbuf(f"q_words{n}", [P, Q], U32)
+            scales = sbuf(f"q_scales{n}", [P, Q], U8)
+            nc.vector.quantize_mx(words[:].bitcast(FP8X4), scales[:], grouped[:].rearrange("p q t -> p (q t)"))
+            q_words.append(words)
+            q_scales.append(scales)
+
+        def scores(n, h, tags):
+            whole = sbuf(f"score{n}{h}", [P, T], F32)
+            rows = slice(h * P, (h + 1) * P)
+            for c in range(T // BANK):
+                acc = bank(f"acc{n}{h}{c}", [P, BANK], *tags[c])
+                nc.tensor.matmul_mx(
+                    acc[:],
+                    lhsT=q_words[n][:, rows].bitcast(FP8X4),
+                    lhsT_scale=q_scales[n][:, rows],
+                    rhs=k_words[c // 2][:, 2 * BANK * (c % 2) : 2 * BANK * (c % 2 + 1)].bitcast(FP4X4),
+                    rhs_scale=k_scales[:, BANK * c : BANK * (c + 1)],
+                    start=True,
+                    stop=True,
+                )
+                nc.scalar.activation(whole[:, BANK * c : BANK * (c + 1)], acc[:], ACT.Copy)
+            return whole
+
+        def gather(out, window, offsets, on_vector):
+            if on_vector:
+                nc.vector.tensor_copy(out, window[:].indirect(offsets[:]))
+            else:
+                nc.scalar.activation(out, window[:].indirect(offsets[:]), ACT.Copy)
+
+        def look_up(name, window, offsets, on_vector):
+            picked = sbuf(name, [P, I], F32)
+            gather(picked[:], window, offsets, on_vector)
+            return picked
+
+
+        def turn_and_add(name, first, second):
+            total = bank(name, [P, PACK, P], name[:3], 2)
+            for c in range(PACK):
+                cols = slice(c * P, (c + 1) * P)
+                nc.tensor.matmul(total[:, c, :], first[:, cols], ident[:], start=True, stop=False, is_transpose=True)
+                nc.tensor.matmul(total[:, c, :], second[:, cols], ident[:], start=False, stop=True, is_transpose=True)
+            return total
+
+        def products(h, a1, a2, b1, b2):
+            aa = sbuf(f"aa{h}", [P, I], F32)
+            bb = sbuf(f"bb{h}", [P, I], F32)
+            ab = sbuf(f"ab{h}", [P, I], F32)
+            ba = sbuf(f"ba{h}", [P, I], F32)
+            nc.vector.tensor_tensor(aa[:], a1[:], a2[:], ALU.mult)
+            nc.vector.tensor_tensor(bb[:], b1[:], b2[:], ALU.mult)
+            dot = turn_and_add(f"dot{h}", aa, bb)
+            nc.vector.tensor_tensor(ab[:], a1[:], b2[:], ALU.mult)
+            nc.vector.scalar_tensor_tensor(ba[:], b1[:], -1.0, a2[:], ALU.mult, ALU.mult)
+            cross = turn_and_add(f"cross{h}", ab, ba)
+            return dot, cross
+
+        def squares(h, dot, cross):
+            d2 = sbuf(f"d2{h}", [P, I], F32)
+            c2 = sbuf(f"c2{h}", [P, I], F32)
+            nc.scalar.activation(d2[:], dot[:].rearrange("s c q -> s (c q)"), ACT.Square)
+            nc.scalar.activation(c2[:], cross[:].rearrange("s c q -> s (c q)"), ACT.Square)
+            den = sbuf(f"den{h}", [P, I], F32)
+            nc.vector.tensor_tensor(den[:], d2[:], c2[:], ALU.add)
+            inv = sbuf(f"inv{h}", [P, PACK, P], F32)
+            nc.scalar.activation(inv[:].rearrange("s c q -> s (c q)"), den[:], ACT.Abs_reciprocal_sqrt, bias=0.5)
+            return inv
+
+        ring = [("ring", 4)] * 4
+        a0 = scores(0, 0, ring)
+        b0 = scores(1, 0, [("dot", 2)] * 2 + [("cro", 2)] * 2)
+        a01 = look_up("a01", a0, list1, True)
+        a02 = look_up("a02", a0, list2, True)
+        a1 = scores(0, 1, ring)
+        b01 = look_up("b01", b0, list1, True)
+        b02 = look_up("b02", b0, list2, True)
+        b1 = scores(1, 1, ring)
+        dot0, cross0 = products(0, a01, a02, b01, b02)
+        a11 = look_up("a11", a1, list1, True)
+        a12 = look_up("a12", a1, list2, False)
+        b11 = look_up("b11", b1, list1, True)
+        b12 = look_up("b12", b1, list2, False)
+        dot1, cross1 = products(1, a11, a12, b11, b12)
+        invs = [squares(0, dot0, cross0), squares(1, dot1, cross1)]
+        dots = [dot0, dot1]
+
+        cos_banks = []
+        for h in range(Q_TILES):
+            cos_t = sbuf(f"cos_t{h}", [P, PACK, P], F32)
+            nc.vector.tensor_tensor(cos_t[:], dots[h][:], invs[h][:], ALU.mult)
+            cos = bank(f"cos{h}", [P, PACK, P], "cro", 2)
+            for c in range(PACK):
+                nc.tensor.transpose(cos[:, c, :], cos_t[:, c, :], ident[:])
+            cos_banks.append(cos)
+
+        v_words = sbuf("v_words", [P, E], U32)
+        v_scales = sbuf("v_scales", [P, E], U8)
+
+        def values(half, on_vector, tags):
+            turned = bank(f"v_turned{half}", [P, 2, 2, P], "ring", 4)
+            for jj in range(2):
+                j = 2 * half + jj
+                picked = sbuf(f"v_picked{j}", [P, I], BF16, tag=tags[jj])
+                gather(picked[:], val_rows[j], list1, on_vector)
+                pairs = picked[:].bitcast(F32)
+                for u in range(2):
+                    nc.tensor.transpose(turned[:, jj, u, :], pairs[:, u : I // 2 : 2], ident[:])
+            grouped = sbuf(f"v_grouped{half}", [P, 2 * P * PACK], BF16)
+            nc.scalar.copy(
+                grouped[:].bitcast(F32).rearrange("s (j e u) -> s j e u", j=2, u=2), turned[:].rearrange("s j u e -> s j e u")
+            )
+            cols = slice(2 * P * half, 2 * P * (half + 1))
+            nc.vector.quantize_mx(v_words[:, cols].bitcast(FP8X4), v_scales[:, cols], grouped[:])
+
+        ps, zs = [], []
+        for h in range(Q_TILES):
+            p = sbuf(f"p{h}", [P, PACK, P], F32, tag=f"den{1 - h}")
+            z0 = sbuf(f"z0{h}", [P, 1], F32)
+            nc.scalar.activation(
+                p[:],
+                cos_banks[h][:].rearrange("q c s -> q (c s)").rearrange("q (s t) -> q t s", t=PACK),
+                ACT.Exp,
+                scale=lam_col[:, h : h + 1],
+                accum_out=z0[:],
+            )
+            ps.append(p)
+            zs.append(z0)
+
+        values(0, True, ("a12", "inv1"))
+        values(1, False, ("cos_t1", "d21"))
+
+        gain = sbuf("gain", [P, Q], F32, tag="c21")
+        gather(gain[:], gain_rows, list3, False)
+        mem = sbuf("mem", [P, PACK, Q], F32, tag="cos_t1")
+        for j in range(PACK):
+            gather(mem[:, j, :], mem_rows[j], list3, False)
+
+        y_words = sbuf("y_words", [P, Q], U32)
+        y_scales = sbuf("y_scales", [P, Q], U8)
+        out_dealt = out_0.rearrange("(p j) q -> p j q", j=PACK)
+        for h in range(Q_TILES):
+            rows = slice(h * P, (h + 1) * P)
+            by_run = ps[h][:].rearrange("q t (g e) -> q t g e", e=RUN // PACK)
+            pg = sbuf(f"pg{h}", [P, G], F32)
+            nc.vector.tensor_reduce(pg[:], by_run.rearrange("q t g e -> q g t e"), AXIS.XY, ALU.add)
+            rest = sbuf(f"rest{h}", [P, G], F32)
+            nc.vector.tensor_scalar(rest[:], pg[:], -1.0, zs[h][:], ALU.mult, ALU.add)
+            k0 = sbuf(f"k0{h}", [P, G], F32)
+            nc.vector.reciprocal(k0[:], rest[:])
+            w = sbuf(f"w{h}", [P, PACK, G, RUN // PACK], F32)
+            nc.vector.tensor_tensor(
+                w[:], by_run, k0[:].unsqueeze(1).unsqueeze(3).to_broadcast([P, PACK, G, RUN // PACK]), ALU.mult
+            )
+            w_turned = bank(f"w_turned{h}", [P, PACK, P], "dot", 2)
+            for t in range(PACK):
+                nc.tensor.transpose(w_turned[:, t, :], w[:, t, :, :].rearrange("q g e -> q (g e)"), ident[:])
+            w_grouped = sbuf(f"w_grouped{h}", [P, P, PACK], BF16)
+            nc.vector.tensor_tensor(
+                w_grouped[:],
+                w_turned[:].rearrange("s t q -> s q t"),
+                os_col[:].unsqueeze(1).to_broadcast([P, P, PACK]),
+                ALU.mult,
+            )
+            w_words = sbuf(f"w_words{h}", [P, P], U32)
+            w_scales = sbuf(f"w_scales{h}", [P, P], U8)
+            nc.vector.quantize_mx(w_words[:].bitcast(FP8X4), w_scales[:], w_grouped[:].rearrange("s q t -> s (q t)"))
+
+            o = bank(f"o{h}", [P, PACK, P], "ring", 4)
+            for j in range(PACK):
+                cols = slice(j * P, (j + 1) * P)
+                nc.tensor.matmul_mx(
+                    o[:, j, :],
+                    lhsT=v_words[:, cols].bitcast(FP8X4),
+                    lhsT_scale=v_scales[:, cols],
+                    rhs=w_words[:].bitcast(FP8X4),
+                    rhs_scale=w_scales[:],
+                    start=True,
+                    stop=True,
+                )
+            scaled = sbuf(f"scaled{h}", [P, PACK, P], F32)
+            nc.vector.tensor_tensor(scaled[:], o[:], gain[:, rows].unsqueeze(1).to_broadcast([P, PACK, P]), ALU.mult)
+            y = sbuf(f"y{h}", [P, PACK, P], F32)
+            nc.vector.tensor_tensor(y[:], scaled[:], mem[:, :, rows], ALU.add)
+            nc.sync.dma_start(out_dealt[:, :, rows], y[:])
+            y_grouped = sbuf(f"y_grouped{h}", [P, P, PACK], BF16)
+            nc.scalar.copy(y_grouped[:], y[:].rearrange("p j q -> p q j"))
+            nc.vector.quantize_mx(
+                y_words[:, rows].bitcast(FP8X4), y_scales[:, rows], y_grouped[:].rearrange("p q j -> p (q j)")
+            )
+
+        nc.sync.dma_start(out_1[0].rearrange("p q j -> p (q j)").bitcast(I32), y_words[:].bitcast(I32))
+        for quad in range(4):
+            engine = nc.scalar if quad % 2 else nc.sync
+            engine.dma_start(
+                out_2[0, 4 * quad : 4 * quad + 4, :].bitcast(I32), y_scales[32 * quad : 32 * quad + 4, :].bitcast(I32)
+            )

@@ -36,8 +36,8 @@ def tile_attend_planecos_outside_bymember_pl_kernel(
         def sbuf(name, shape, dtype, tag=None):
             return keep.tile(shape, dtype, name=name, tag=tag or name, align_bytes=64)
 
-        def bank(name, shape, tag, bufs):
-            return psum.tile(shape, F32, name=name, tag=tag, bufs=bufs)
+        def bank(name, shape, tag):
+            return psum.tile(shape, F32, name=name, tag=f"bank{tag}")
 
         q_raw = [sbuf(f"q_raw{n}", [P, PACK, Q], F32) for n in range(2)]
         k_words = [sbuf(f"k_words{n}", [P, T], U8) for n in range(2)]
@@ -52,21 +52,20 @@ def tile_attend_planecos_outside_bymember_pl_kernel(
         gain_rows = sbuf("gain_rows", [P, M], F32)
 
         nc.sync.dma_start(q_raw[0][:], query.rearrange("(p j) q -> p j q", j=PACK))
+        for r in range(4):
+            engine = nc.scalar if r else nc.sync
+            engine.dma_start(k_scales[r:P:32, :].bitcast(I32), keys_scales[0, r:16:4, :].bitcast(I32))
         nc.sync.dma_start(k_words[0][:].bitcast(I32), keys_words[0, :, :T].bitcast(I32))
-        for quad in range(4):
-            nc.sync.dma_start(
-                k_scales[32 * quad : 32 * quad + 4, :].bitcast(I32), keys_scales[0, 4 * quad : 4 * quad + 4, :].bitcast(I32)
-            )
         nc.sync.dma_start(k_words[1][:].bitcast(I32), keys_words[0, :, T:].bitcast(I32))
         nc.sync.dma_start(q_raw[1][:], query2.rearrange("(p j) q -> p j q", j=PACK))
         nc.sync.dma_start(list1[:], offs)
         nc.sync.dma_start(list2[:], offs2)
-        vals_dealt = vals.rearrange("(p j) t -> p j t", j=PACK)
-        for j in range(PACK):
-            nc.sync.dma_start(val_rows[j][:], vals_dealt[:, j, :])
         with nc.allow_non_contiguous_dma(reason="one score factor a partition"):
             nc.sync.dma_start(lam_col[:], lam.rearrange("(h p) o -> p (h o)", p=P))
         nc.sync.dma_start(os_col[:], slot_factor.rearrange("o (p t) -> p (o t)", t=PACK))
+        vals_dealt = vals.rearrange("(p j) t -> p j t", j=PACK)
+        for j in range(PACK):
+            nc.sync.dma_start(val_rows[j][:], vals_dealt[:, j, :])
         nc.sync.dma_start(list3[:], offs3)
         nc.sync.dma_start(gain_rows[:], mgain)
         member_dealt = member.rearrange("(p j) m -> p j m", j=PACK)
@@ -75,6 +74,9 @@ def tile_attend_planecos_outside_bymember_pl_kernel(
 
         ident = sbuf("ident", [P, P], F32)
         make_identity(nc, ident[:])
+
+        warm = sbuf("warm", [P, 1], F32)
+        nc.scalar.activation(warm[:], ident[:, 0:1], ACT.Abs_reciprocal_sqrt, bias=0.5)
 
         q_words, q_scales = [], []
         for n in range(2):
@@ -88,11 +90,11 @@ def tile_attend_planecos_outside_bymember_pl_kernel(
             q_words.append(words)
             q_scales.append(scales)
 
-        def scores(n, h, tags):
+        def scores(n, h, tag, on_vector):
             whole = sbuf(f"score{n}{h}", [P, T], F32)
             rows = slice(h * P, (h + 1) * P)
             for c in range(T // BANK):
-                acc = bank(f"acc{n}{h}{c}", [P, BANK], *tags[c])
+                acc = bank(f"acc{n}{h}{c}", [P, BANK], tag + c)
                 nc.tensor.matmul_mx(
                     acc[:],
                     lhsT=q_words[n][:, rows].bitcast(FP8X4),
@@ -102,89 +104,116 @@ def tile_attend_planecos_outside_bymember_pl_kernel(
                     start=True,
                     stop=True,
                 )
-                nc.scalar.activation(whole[:, BANK * c : BANK * (c + 1)], acc[:], ACT.Copy)
+                if c in on_vector:
+                    nc.vector.tensor_copy(whole[:, BANK * c : BANK * (c + 1)], acc[:])
+                else:
+                    nc.scalar.activation(whole[:, BANK * c : BANK * (c + 1)], acc[:], ACT.Copy)
             return whole
 
         def gather(out, window, offsets, on_vector):
             if on_vector:
-                nc.vector.tensor_copy(out, window[:].indirect(offsets[:]))
+                nc.vector.tensor_copy(out, window[:].indirect(offsets))
             else:
-                nc.scalar.activation(out, window[:].indirect(offsets[:]), ACT.Copy)
+                nc.scalar.activation(out, window[:].indirect(offsets), ACT.Copy)
 
-        def look_up(name, window, offsets, on_vector):
-            picked = sbuf(name, [P, I], F32)
-            gather(picked[:], window, offsets, on_vector)
+        def look_up(name, window, offsets, on_vector, pieces=1, tag=None):
+            picked = sbuf(name, [P, I], F32, tag=tag)
+            width = I // pieces
+            for n in range(pieces):
+                gather(picked[:, n * width : (n + 1) * width], window, offsets[:, n * width // 16 : (n + 1) * width // 16], on_vector)
             return picked
 
+        seen = {}
 
-        def turn_and_add(name, first, second):
-            total = bank(name, [P, PACK, P], name[:3], 2)
-            for c in range(PACK):
-                cols = slice(c * P, (c + 1) * P)
-                nc.tensor.matmul(total[:, c, :], first[:, cols], ident[:], start=True, stop=False, is_transpose=True)
-                nc.tensor.matmul(total[:, c, :], second[:, cols], ident[:], start=False, stop=True, is_transpose=True)
-            return total
-
-        def products(h, a1, a2, b1, b2):
+        def products(h, a1, a2, b1, b2, pieces):
             aa = sbuf(f"aa{h}", [P, I], F32)
+            ba = sbuf(f"ba{h}", [P, I], F32)
             bb = sbuf(f"bb{h}", [P, I], F32)
             ab = sbuf(f"ab{h}", [P, I], F32)
-            ba = sbuf(f"ba{h}", [P, I], F32)
             nc.vector.tensor_tensor(aa[:], a1[:], a2[:], ALU.mult)
-            nc.vector.tensor_tensor(bb[:], b1[:], b2[:], ALU.mult)
-            dot = turn_and_add(f"dot{h}", aa, bb)
-            nc.vector.tensor_tensor(ab[:], a1[:], b2[:], ALU.mult)
             nc.vector.scalar_tensor_tensor(ba[:], b1[:], -1.0, a2[:], ALU.mult, ALU.mult)
-            cross = turn_and_add(f"cross{h}", ab, ba)
-            return dot, cross
+            width = I // pieces
+            for n in range(pieces):
+                cols = slice(n * width, (n + 1) * width)
+                nc.vector.tensor_tensor(bb[:, cols], b1[:, cols], b2[:, cols], ALU.mult)
+                nc.vector.tensor_tensor(ab[:, cols], a1[:, cols], b2[:, cols], ALU.mult)
+            seen[h] = (aa, ba, bb, ab)
+            sums = []
+            for half in range(2):
+                both = bank(f"both{h}{half}", [P, 2, 2, P], 2 * h + half)
+                terms = [(0, aa), (1, ba), (0, bb), (1, ab)]
+                for n, (which, term) in enumerate(terms):
+                    for c in range(2):
+                        cols = slice((2 * half + c) * P, (2 * half + c + 1) * P)
+                        nc.tensor.matmul(
+                            both[:, which, c, :],
+                            term[:, cols],
+                            ident[:],
+                            start=(n == 0 and c == 0),
+                            stop=(n == len(terms) - 1 and c == 1),
+                            is_transpose=True,
+                        )
+                sums.append(both)
+            return sums
 
-        def squares(h, dot, cross):
-            d2 = sbuf(f"d2{h}", [P, I], F32)
-            c2 = sbuf(f"c2{h}", [P, I], F32)
-            nc.scalar.activation(d2[:], dot[:].rearrange("s c q -> s (c q)"), ACT.Square)
-            nc.scalar.activation(c2[:], cross[:].rearrange("s c q -> s (c q)"), ACT.Square)
-            den = sbuf(f"den{h}", [P, I], F32)
-            nc.vector.tensor_tensor(den[:], d2[:], c2[:], ALU.add)
-            inv = sbuf(f"inv{h}", [P, PACK, P], F32)
+        def inverse_root(name, both):
+            squares = sbuf(f"squares{name}", [P, 2, 2 * P], F32)
+            nc.scalar.activation(squares[:], both[:].rearrange("s w c q -> s w (c q)"), ACT.Square)
+            den = sbuf(f"den{name}", [P, 2 * P], F32)
+            nc.vector.tensor_tensor(den[:], squares[:, 0, :], squares[:, 1, :], ALU.add)
+            inv = sbuf(f"inv{name}", [P, 2, P], F32)
             nc.scalar.activation(inv[:].rearrange("s c q -> s (c q)"), den[:], ACT.Abs_reciprocal_sqrt, bias=0.5)
             return inv
 
-        ring = [("ring", 4)] * 4
-        a0 = scores(0, 0, ring)
-        b0 = scores(1, 0, [("dot", 2)] * 2 + [("cro", 2)] * 2)
-        a01 = look_up("a01", a0, list1, True)
+        a0 = scores(0, 0, 4, ())
+        b0 = scores(1, 0, 0, ())
+        a01 = look_up("a01", a0, list1, True, tag="q_grouped1")
         a02 = look_up("a02", a0, list2, True)
-        a1 = scores(0, 1, ring)
+        a1 = scores(0, 1, 0, ())
         b01 = look_up("b01", b0, list1, True)
         b02 = look_up("b02", b0, list2, True)
-        b1 = scores(1, 1, ring)
-        dot0, cross0 = products(0, a01, a02, b01, b02)
-        a11 = look_up("a11", a1, list1, True)
+        b1 = scores(1, 1, 0, ())
+        sums = [products(0, a01, a02, b01, b02, 1)]
         a12 = look_up("a12", a1, list2, False)
+        a11 = look_up("a11", a1, list1, True)
         b11 = look_up("b11", b1, list1, True)
-        b12 = look_up("b12", b1, list2, False)
-        dot1, cross1 = products(1, a11, a12, b11, b12)
-        invs = [squares(0, dot0, cross0), squares(1, dot1, cross1)]
-        dots = [dot0, dot1]
+        b12 = look_up("b12", b1, list2, False, 2)
+        sums.append(products(1, a11, a12, b11, b12, 2))
+        invs = [[inverse_root(f"{h}{half}", sums[h][half]) for half in range(2)] for h in range(Q_TILES)]
 
         cos_banks = []
         for h in range(Q_TILES):
-            cos_t = sbuf(f"cos_t{h}", [P, PACK, P], F32)
-            nc.vector.tensor_tensor(cos_t[:], dots[h][:], invs[h][:], ALU.mult)
-            cos = bank(f"cos{h}", [P, PACK, P], "cro", 2)
-            for c in range(PACK):
-                nc.tensor.transpose(cos[:, c, :], cos_t[:, c, :], ident[:])
+            cos = bank(f"cos{h}", [P, PACK, P], 5 + h)
+            for half in range(2):
+                cos_t = sbuf(f"cos_t{h}{half}", [P, 2, P], F32)
+                nc.vector.tensor_tensor(cos_t[:], sums[h][half][:, 0, :, :], invs[h][half][:], ALU.mult)
+                for c in range(2):
+                    nc.tensor.transpose(cos[:, 2 * half + c, :], cos_t[:, c, :], ident[:])
             cos_banks.append(cos)
+
+        os_rows = bank("os_rows", [P, PACK, P], 4)
+        for t in range(PACK):
+            nc.tensor.transpose(os_rows[:, t, :], os_col[:, t : t + 1].to_broadcast([P, P]), ident[:])
+
+        ps, zs = [], []
+        for h in range(Q_TILES):
+            p = sbuf(f"p{h}", [P, I], F32, tag=f"den1{1 - h}")
+            z0 = sbuf(f"z0{h}", [P, 1], F32)
+            nc.scalar.activation(
+                p[:], cos_banks[h][:].rearrange("q c s -> q (c s)"), ACT.Exp, scale=lam_col[:, h : h + 1], accum_out=z0[:]
+            )
+            ps.append(p)
+            zs.append(z0)
 
         v_words = sbuf("v_words", [P, E], U32)
         v_scales = sbuf("v_scales", [P, E], U8)
 
         def values(half, on_vector, tags):
-            turned = bank(f"v_turned{half}", [P, 2, 2, P], "ring", 4)
+            turned = bank(f"v_turned{half}", [P, 2, 2, P], half)
             for jj in range(2):
                 j = 2 * half + jj
                 picked = sbuf(f"v_picked{j}", [P, I], BF16, tag=tags[jj])
-                gather(picked[:], val_rows[j], list1, on_vector)
+                gather(picked[:], val_rows[j], list1[:], on_vector[jj])
                 pairs = picked[:].bitcast(F32)
                 for u in range(2):
                     nc.tensor.transpose(turned[:, jj, u, :], pairs[:, u : I // 2 : 2], ident[:])
@@ -195,60 +224,54 @@ def tile_attend_planecos_outside_bymember_pl_kernel(
             cols = slice(2 * P * half, 2 * P * (half + 1))
             nc.vector.quantize_mx(v_words[:, cols].bitcast(FP8X4), v_scales[:, cols], grouped[:])
 
-        ps, zs = [], []
+        values(0, (False, True), ("ab0", "inv11"))
+        values(1, (True, False), ("b12", "cos_t11"))
+        gain = sbuf("gain", [P, Q], F32, tag="inv10")
+        gather(gain[:], gain_rows, list3[:], True)
+
+        w_quantised = []
+        ws = []
         for h in range(Q_TILES):
-            p = sbuf(f"p{h}", [P, PACK, P], F32, tag=f"den{1 - h}")
-            z0 = sbuf(f"z0{h}", [P, 1], F32)
-            nc.scalar.activation(
-                p[:],
-                cos_banks[h][:].rearrange("q c s -> q (c s)").rearrange("q (s t) -> q t s", t=PACK),
-                ACT.Exp,
-                scale=lam_col[:, h : h + 1],
-                accum_out=z0[:],
+            pg = sbuf(f"pg{h}", [P, G], F32)
+            nc.vector.tensor_reduce(pg[:], ps[h][:].rearrange("q (g e) -> q g e", e=RUN), AXIS.X, ALU.add)
+            p_os = sbuf(f"p_os{h}", [P, I], F32)
+            nc.vector.tensor_tensor(
+                p_os[:].rearrange("q (s t) -> q s t", t=PACK),
+                ps[h][:].rearrange("q (s t) -> q s t", t=PACK),
+                os_rows[:].rearrange("q t s -> q s t"),
+                ALU.mult,
             )
-            ps.append(p)
-            zs.append(z0)
-
-        values(0, True, ("a12", "inv1"))
-        values(1, False, ("cos_t1", "d21"))
-
-        gain = sbuf("gain", [P, Q], F32, tag="c21")
-        gather(gain[:], gain_rows, list3, False)
-        mem = sbuf("mem", [P, PACK, Q], F32, tag="cos_t1")
-        for j in range(PACK):
-            gather(mem[:, j, :], mem_rows[j], list3, False)
+            rest = sbuf(f"rest{h}", [P, G], F32)
+            nc.vector.tensor_scalar(rest[:], pg[:], -1.0, zs[h][:], ALU.mult, ALU.add)
+            k0 = sbuf(f"k0{h}", [P, G], F32)
+            nc.vector.reciprocal(k0[:], rest[:])
+            w = sbuf(f"w{h}", [P, I], BF16)
+            nc.vector.tensor_tensor(
+                w[:].rearrange("q (g e) -> q g e", e=RUN),
+                p_os[:].rearrange("q (g e) -> q g e", e=RUN),
+                k0[:].unsqueeze(2).to_broadcast([P, G, RUN]),
+                ALU.mult,
+            )
+            w_turned = bank(f"w_turned{h}", [P, 2, P], 5 + h)
+            pairs = w[:].bitcast(F32)
+            for u in range(2):
+                nc.tensor.transpose(w_turned[:, u, :], pairs[:, u : I // 2 : 2], ident[:])
+            w_grouped = sbuf(f"w_grouped{h}", [P, P * PACK], BF16)
+            nc.scalar.copy(w_grouped[:].bitcast(F32).rearrange("s (q u) -> s q u", u=2), w_turned[:].rearrange("s u q -> s q u"))
+            w_words = sbuf(f"w_words{h}", [P, P], U32)
+            w_scales = sbuf(f"w_scales{h}", [P, P], U8)
+            nc.vector.quantize_mx(w_words[:].bitcast(FP8X4), w_scales[:], w_grouped[:])
+            w_quantised.append((w_words, w_scales))
 
         y_words = sbuf("y_words", [P, Q], U32)
         y_scales = sbuf("y_scales", [P, Q], U8)
         out_dealt = out_0.rearrange("(p j) q -> p j q", j=PACK)
         for h in range(Q_TILES):
-            rows = slice(h * P, (h + 1) * P)
-            by_run = ps[h][:].rearrange("q t (g e) -> q t g e", e=RUN // PACK)
-            pg = sbuf(f"pg{h}", [P, G], F32)
-            nc.vector.tensor_reduce(pg[:], by_run.rearrange("q t g e -> q g t e"), AXIS.XY, ALU.add)
-            rest = sbuf(f"rest{h}", [P, G], F32)
-            nc.vector.tensor_scalar(rest[:], pg[:], -1.0, zs[h][:], ALU.mult, ALU.add)
-            k0 = sbuf(f"k0{h}", [P, G], F32)
-            nc.vector.reciprocal(k0[:], rest[:])
-            w = sbuf(f"w{h}", [P, PACK, G, RUN // PACK], F32)
-            nc.vector.tensor_tensor(
-                w[:], by_run, k0[:].unsqueeze(1).unsqueeze(3).to_broadcast([P, PACK, G, RUN // PACK]), ALU.mult
-            )
-            w_turned = bank(f"w_turned{h}", [P, PACK, P], "dot", 2)
-            for t in range(PACK):
-                nc.tensor.transpose(w_turned[:, t, :], w[:, t, :, :].rearrange("q g e -> q (g e)"), ident[:])
-            w_grouped = sbuf(f"w_grouped{h}", [P, P, PACK], BF16)
-            nc.vector.tensor_tensor(
-                w_grouped[:],
-                w_turned[:].rearrange("s t q -> s q t"),
-                os_col[:].unsqueeze(1).to_broadcast([P, P, PACK]),
-                ALU.mult,
-            )
-            w_words = sbuf(f"w_words{h}", [P, P], U32)
-            w_scales = sbuf(f"w_scales{h}", [P, P], U8)
-            nc.vector.quantize_mx(w_words[:].bitcast(FP8X4), w_scales[:], w_grouped[:].rearrange("s q t -> s (q t)"))
-
-            o = bank(f"o{h}", [P, PACK, P], "ring", 4)
+            w_words, w_scales = w_quantised[h]
+            mem = sbuf(f"mem{h}", [P, PACK, P], F32, tag=("cos_t11", "w1")[h])
+            for j in range(PACK):
+                gather(mem[:, j, :], mem_rows[j], list3[:, h * P // 16 : (h + 1) * P // 16], False)
+            o = bank(f"o{h}", [P, PACK, P], 2 + h)
             for j in range(PACK):
                 cols = slice(j * P, (j + 1) * P)
                 nc.tensor.matmul_mx(
@@ -261,19 +284,27 @@ def tile_attend_planecos_outside_bymember_pl_kernel(
                     stop=True,
                 )
             scaled = sbuf(f"scaled{h}", [P, PACK, P], F32)
-            nc.vector.tensor_tensor(scaled[:], o[:], gain[:, rows].unsqueeze(1).to_broadcast([P, PACK, P]), ALU.mult)
             y = sbuf(f"y{h}", [P, PACK, P], F32)
-            nc.vector.tensor_tensor(y[:], scaled[:], mem[:, :, rows], ALU.add)
-            nc.sync.dma_start(out_dealt[:, :, rows], y[:])
             y_grouped = sbuf(f"y_grouped{h}", [P, P, PACK], BF16)
-            nc.scalar.copy(y_grouped[:], y[:].rearrange("p j q -> p q j"))
-            nc.vector.quantize_mx(
-                y_words[:, rows].bitcast(FP8X4), y_scales[:, rows], y_grouped[:].rearrange("p q j -> p (q j)")
-            )
+            width = P // (h + 1)
+            pieces = [slice(start, start + width) for start in range(0, P, width)]
+            for cols in pieces:
+                rows = slice(h * P + cols.start, h * P + cols.stop)
+                nc.vector.tensor_tensor(
+                    scaled[:, :, cols], o[:, :, cols], gain[:, rows].unsqueeze(1).to_broadcast([P, PACK, width]), ALU.mult
+                )
+            for cols in pieces:
+                rows = slice(h * P + cols.start, h * P + cols.stop)
+                nc.vector.tensor_tensor(y[:, :, cols], scaled[:, :, cols], mem[:, :, cols], ALU.add)
+                nc.scalar.copy(y_grouped[:, cols, :], y[:, :, cols].rearrange("p j q -> p q j"))
+            for cols in pieces:
+                rows = slice(h * P + cols.start, h * P + cols.stop)
+                nc.vector.quantize_mx(
+                    y_words[:, rows].bitcast(FP8X4), y_scales[:, rows], y_grouped[:, cols, :].rearrange("p q j -> p (q j)")
+                )
+            nc.sync.dma_start(out_dealt[:, :, h * P : (h + 1) * P], y[:])
 
         nc.sync.dma_start(out_1[0].rearrange("p q j -> p (q j)").bitcast(I32), y_words[:].bitcast(I32))
-        for quad in range(4):
-            engine = nc.scalar if quad % 2 else nc.sync
-            engine.dma_start(
-                out_2[0, 4 * quad : 4 * quad + 4, :].bitcast(I32), y_scales[32 * quad : 32 * quad + 4, :].bitcast(I32)
-            )
+        for r in range(4):
+            engine = nc.scalar if r % 2 else nc.sync
+            engine.dma_start(out_2[0, r:16:4, :].bitcast(I32), y_scales[r:P:32, :].bitcast(I32))

@@ -58,6 +58,8 @@ def tile_attend_planecos_outside_bymember_pl_kernel(
         nc.sync.dma_start(k_words[0][:].bitcast(I32), keys_words[0, :, :T].bitcast(I32))
         nc.sync.dma_start(k_words[1][:].bitcast(I32), keys_words[0, :, T:].bitcast(I32))
         nc.sync.dma_start(q_raw[1][:], query2.rearrange("(p j) q -> p j q", j=PACK))
+        nc.sync.dma_start(list3[:], offs3)
+        nc.sync.dma_start(gain_rows[:], mgain)
         nc.sync.dma_start(list1[:], offs)
         nc.sync.dma_start(list2[:], offs2)
         with nc.allow_non_contiguous_dma(reason="one score factor a partition"):
@@ -66,8 +68,6 @@ def tile_attend_planecos_outside_bymember_pl_kernel(
         vals_dealt = vals.rearrange("(p j) t -> p j t", j=PACK)
         for j in range(PACK):
             nc.sync.dma_start(val_rows[j][:], vals_dealt[:, j, :])
-        nc.sync.dma_start(list3[:], offs3)
-        nc.sync.dma_start(gain_rows[:], mgain)
         member_dealt = member.rearrange("(p j) m -> p j m", j=PACK)
         for j in range(PACK):
             nc.sync.dma_start(mem_rows[j][:], member_dealt[:, j, :])
@@ -125,18 +125,21 @@ def tile_attend_planecos_outside_bymember_pl_kernel(
 
         seen = {}
 
-        def products(h, a1, a2, b1, b2, pieces):
-            aa = sbuf(f"aa{h}", [P, I], F32)
+        def minus_ba(h, a2, b1):
             ba = sbuf(f"ba{h}", [P, I], F32)
+            nc.vector.scalar_tensor_tensor(ba[:], b1[:], -1.0, a2[:], ALU.mult, ALU.mult)
+            return ba
+
+        def products(h, a1, a2, b1, b2, ba, engine, pieces):
+            aa = sbuf(f"aa{h}", [P, I], F32)
             bb = sbuf(f"bb{h}", [P, I], F32)
             ab = sbuf(f"ab{h}", [P, I], F32)
-            nc.vector.tensor_tensor(aa[:], a1[:], a2[:], ALU.mult)
-            nc.vector.scalar_tensor_tensor(ba[:], b1[:], -1.0, a2[:], ALU.mult, ALU.mult)
+            nc.gpsimd.tensor_tensor(aa[:], a1[:], a2[:], ALU.mult)
             width = I // pieces
             for n in range(pieces):
                 cols = slice(n * width, (n + 1) * width)
-                nc.vector.tensor_tensor(bb[:, cols], b1[:, cols], b2[:, cols], ALU.mult)
-                nc.vector.tensor_tensor(ab[:, cols], a1[:, cols], b2[:, cols], ALU.mult)
+                engine.tensor_tensor(bb[:, cols], b1[:, cols], b2[:, cols], ALU.mult)
+                engine.tensor_tensor(ab[:, cols], a1[:, cols], b2[:, cols], ALU.mult)
             seen[h] = (aa, ba, bb, ab)
             sums = []
             for half in range(2):
@@ -165,20 +168,23 @@ def tile_attend_planecos_outside_bymember_pl_kernel(
             nc.scalar.activation(inv[:].rearrange("s c q -> s (c q)"), den[:], ACT.Abs_reciprocal_sqrt, bias=0.5)
             return inv
 
-        a0 = scores(0, 0, 4, ())
+        a0 = scores(0, 0, 4, (3,))
         b0 = scores(1, 0, 0, ())
-        a01 = look_up("a01", a0, list1, True, tag="q_grouped1")
+        gain = sbuf("gain", [P, Q], F32, tag="q_grouped1")
+        gather(gain[:], gain_rows, list3[:], True)
+        a01 = look_up("a01", a0, list1, True, tag="q_raw1")
         a02 = look_up("a02", a0, list2, True)
         a1 = scores(0, 1, 0, ())
         b01 = look_up("b01", b0, list1, True)
+        ba0 = minus_ba(0, a02, b01)
         b02 = look_up("b02", b0, list2, True)
         b1 = scores(1, 1, 0, ())
-        sums = [products(0, a01, a02, b01, b02, 1)]
-        a12 = look_up("a12", a1, list2, False)
+        sums = [products(0, a01, a02, b01, b02, ba0, nc.gpsimd, 1)]
         a11 = look_up("a11", a1, list1, True)
+        a12 = look_up("a12", a1, list2, True)
         b11 = look_up("b11", b1, list1, True)
         b12 = look_up("b12", b1, list2, False, 2)
-        sums.append(products(1, a11, a12, b11, b12, 2))
+        sums.append(products(1, a11, a12, b11, b12, minus_ba(1, a12, b11), nc.vector, 2))
         invs = [[inverse_root(f"{h}{half}", sums[h][half]) for half in range(2)] for h in range(Q_TILES)]
 
         cos_banks = []
@@ -226,8 +232,6 @@ def tile_attend_planecos_outside_bymember_pl_kernel(
 
         values(0, (False, True), ("ab0", "inv11"))
         values(1, (True, False), ("b12", "cos_t11"))
-        gain = sbuf("gain", [P, Q], F32, tag="inv10")
-        gather(gain[:], gain_rows, list3[:], True)
 
         w_quantised = []
         ws = []

@@ -46,7 +46,7 @@ def tile_attend_planecos_outside_bymember_pl_kernel(
         list2 = keep.tile([P, I // 16], U16, name="list2")
         list3 = keep.tile([P, Q // 16], U16, name="list3")
         lam_col = sbuf("lam_col", [P, Q_TILES], F32)
-        os_col = sbuf("os_col", [P, PACK], F32)
+        os_rows = sbuf("os_rows", [P, I], F32)
         val_rows = [sbuf(f"val_rows{j}", [P, T], F32) for j in range(PACK)]
         mem_rows = [sbuf(f"mem_rows{j}", [P, M], F32) for j in range(PACK)]
         gain_rows = sbuf("gain_rows", [P, M], F32)
@@ -64,13 +64,14 @@ def tile_attend_planecos_outside_bymember_pl_kernel(
         nc.sync.dma_start(list2[:], offs2)
         with nc.allow_non_contiguous_dma(reason="one score factor a partition"):
             nc.sync.dma_start(lam_col[:], lam.rearrange("(h p) o -> p (h o)", p=P))
-        nc.sync.dma_start(os_col[:], slot_factor.rearrange("o (p t) -> p (o t)", t=PACK))
         vals_dealt = vals.rearrange("(p j) t -> p j t", j=PACK)
-        for j in range(PACK):
+        for j in (0, 2, 1):
             nc.sync.dma_start(val_rows[j][:], vals_dealt[:, j, :])
         member_dealt = member.rearrange("(p j) m -> p j m", j=PACK)
         for j in range(PACK):
             nc.sync.dma_start(mem_rows[j][:], member_dealt[:, j, :])
+        nc.sync.dma_start(val_rows[3][:], vals_dealt[:, 3, :])
+        nc.sync.dma_start(os_rows[:], slot_factor[0].partition_broadcast(P))
 
         ident = sbuf("ident", [P, P], F32)
         make_identity(nc, ident[:])
@@ -159,16 +160,16 @@ def tile_attend_planecos_outside_bymember_pl_kernel(
                 sums.append(both)
             return sums
 
-        def inverse_root(name, both):
+        def inverse_root(name, both, engine):
             squares = sbuf(f"squares{name}", [P, 2, 2 * P], F32)
             nc.scalar.activation(squares[:], both[:].rearrange("s w c q -> s w (c q)"), ACT.Square)
             den = sbuf(f"den{name}", [P, 2 * P], F32)
-            nc.vector.tensor_tensor(den[:], squares[:, 0, :], squares[:, 1, :], ALU.add)
+            engine.tensor_tensor(den[:], squares[:, 0, :], squares[:, 1, :], ALU.add)
             inv = sbuf(f"inv{name}", [P, 2, P], F32)
             nc.scalar.activation(inv[:].rearrange("s c q -> s (c q)"), den[:], ACT.Abs_reciprocal_sqrt, bias=0.5)
             return inv
 
-        a0 = scores(0, 0, 4, (3,))
+        a0 = scores(0, 0, 4, ())
         b0 = scores(1, 0, 0, ())
         gain = sbuf("gain", [P, Q], F32, tag="q_grouped1")
         gather(gain[:], gain_rows, list3[:], True)
@@ -185,7 +186,7 @@ def tile_attend_planecos_outside_bymember_pl_kernel(
         b11 = look_up("b11", b1, list1, True)
         b12 = look_up("b12", b1, list2, False, 2)
         sums.append(products(1, a11, a12, b11, b12, minus_ba(1, a12, b11), nc.vector, 2))
-        invs = [[inverse_root(f"{h}{half}", sums[h][half]) for half in range(2)] for h in range(Q_TILES)]
+        invs = [[inverse_root(f"{h}{half}", sums[h][half], (nc.gpsimd, nc.vector)[h]) for half in range(2)] for h in range(Q_TILES)]
 
         cos_banks = []
         for h in range(Q_TILES):
@@ -197,10 +198,6 @@ def tile_attend_planecos_outside_bymember_pl_kernel(
                     nc.tensor.transpose(cos[:, 2 * half + c, :], cos_t[:, c, :], ident[:])
             cos_banks.append(cos)
 
-        os_rows = bank("os_rows", [P, PACK, P], 4)
-        for t in range(PACK):
-            nc.tensor.transpose(os_rows[:, t, :], os_col[:, t : t + 1].to_broadcast([P, P]), ident[:])
-
         ps, zs = [], []
         for h in range(Q_TILES):
             p = sbuf(f"p{h}", [P, I], F32, tag=f"den1{1 - h}")
@@ -210,9 +207,6 @@ def tile_attend_planecos_outside_bymember_pl_kernel(
             )
             ps.append(p)
             zs.append(z0)
-
-        v_words = sbuf("v_words", [P, E], U32)
-        v_scales = sbuf("v_scales", [P, E], U8)
 
         def values(half, on_vector, tags):
             turned = bank(f"v_turned{half}", [P, 2, 2, P], half)
@@ -227,44 +221,49 @@ def tile_attend_planecos_outside_bymember_pl_kernel(
             nc.scalar.copy(
                 grouped[:].bitcast(F32).rearrange("s (j e u) -> s j e u", j=2, u=2), turned[:].rearrange("s j u e -> s j e u")
             )
-            cols = slice(2 * P * half, 2 * P * (half + 1))
-            nc.vector.quantize_mx(v_words[:, cols].bitcast(FP8X4), v_scales[:, cols], grouped[:])
+            return grouped
 
-        values(0, (False, True), ("ab0", "inv11"))
-        values(1, (True, False), ("b12", "cos_t11"))
+        v_grouped = [values(0, (False, True), ("b01", "inv11")), values(1, (True, False), ("b12", "cos_t11"))]
 
-        w_quantised = []
-        ws = []
-        for h in range(Q_TILES):
-            pg = sbuf(f"pg{h}", [P, G], F32)
-            nc.vector.tensor_reduce(pg[:], ps[h][:].rearrange("q (g e) -> q g e", e=RUN), AXIS.X, ALU.add)
-            p_os = sbuf(f"p_os{h}", [P, I], F32)
-            nc.vector.tensor_tensor(
-                p_os[:].rearrange("q (s t) -> q s t", t=PACK),
-                ps[h][:].rearrange("q (s t) -> q s t", t=PACK),
-                os_rows[:].rearrange("q t s -> q s t"),
-                ALU.mult,
-            )
-            rest = sbuf(f"rest{h}", [P, G], F32)
-            nc.vector.tensor_scalar(rest[:], pg[:], -1.0, zs[h][:], ALU.mult, ALU.add)
-            k0 = sbuf(f"k0{h}", [P, G], F32)
-            nc.vector.reciprocal(k0[:], rest[:])
+        tiles = range(Q_TILES)
+        pg = [sbuf(f"pg{h}", [P, G], F32) for h in tiles]
+        rest = [sbuf(f"rest{h}", [P, G], F32) for h in tiles]
+        k0 = [sbuf(f"k0{h}", [P, G], F32) for h in tiles]
+        for h in tiles:
+            nc.vector.tensor_reduce(pg[h][:], ps[h][:].rearrange("q (g e) -> q g e", e=RUN), AXIS.X, ALU.add)
+        for h in tiles:
+            nc.vector.tensor_scalar(rest[h][:], pg[h][:], -1.0, zs[h][:], ALU.mult, ALU.add)
+        for h in tiles:
+            nc.vector.reciprocal(k0[h][:], rest[h][:])
+        w_grouped = []
+        for h in tiles:
+            p_os = sbuf(f"p_os{h}", [P, I], F32, tag=("p_os0", "pg1")[h])
+            nc.gpsimd.tensor_tensor(p_os[:], ps[h][:], os_rows[:], ALU.mult)
             w = sbuf(f"w{h}", [P, I], BF16)
             nc.vector.tensor_tensor(
                 w[:].rearrange("q (g e) -> q g e", e=RUN),
                 p_os[:].rearrange("q (g e) -> q g e", e=RUN),
-                k0[:].unsqueeze(2).to_broadcast([P, G, RUN]),
+                k0[h][:].unsqueeze(2).to_broadcast([P, G, RUN]),
                 ALU.mult,
             )
             w_turned = bank(f"w_turned{h}", [P, 2, P], 5 + h)
             pairs = w[:].bitcast(F32)
             for u in range(2):
                 nc.tensor.transpose(w_turned[:, u, :], pairs[:, u : I // 2 : 2], ident[:])
-            w_grouped = sbuf(f"w_grouped{h}", [P, P * PACK], BF16)
-            nc.scalar.copy(w_grouped[:].bitcast(F32).rearrange("s (q u) -> s q u", u=2), w_turned[:].rearrange("s u q -> s q u"))
+            grouped = sbuf(f"w_grouped{h}", [P, P * PACK], BF16)
+            nc.scalar.copy(grouped[:].bitcast(F32).rearrange("s (q u) -> s q u", u=2), w_turned[:].rearrange("s u q -> s q u"))
+            w_grouped.append(grouped)
+
+        v_words = sbuf("v_words", [P, E], U32, tag="pg1")
+        v_scales = sbuf("v_scales", [P, E], U8)
+        for half in range(2):
+            cols = slice(2 * P * half, 2 * P * (half + 1))
+            nc.vector.quantize_mx(v_words[:, cols].bitcast(FP8X4), v_scales[:, cols], v_grouped[half][:])
+        w_quantised = []
+        for h in tiles:
             w_words = sbuf(f"w_words{h}", [P, P], U32)
             w_scales = sbuf(f"w_scales{h}", [P, P], U8)
-            nc.vector.quantize_mx(w_words[:].bitcast(FP8X4), w_scales[:], w_grouped[:])
+            nc.vector.quantize_mx(w_words[:].bitcast(FP8X4), w_scales[:], w_grouped[h][:])
             w_quantised.append((w_words, w_scales))
 
         y_words = sbuf("y_words", [P, Q], U32)
@@ -272,9 +271,9 @@ def tile_attend_planecos_outside_bymember_pl_kernel(
         out_dealt = out_0.rearrange("(p j) q -> p j q", j=PACK)
         for h in range(Q_TILES):
             w_words, w_scales = w_quantised[h]
-            mem = sbuf(f"mem{h}", [P, PACK, P], F32, tag=("cos_t11", "w1")[h])
+            mem = sbuf(f"mem{h}", [P, PACK, P], F32, tag=("inv10", "w1")[h])
             for j in range(PACK):
-                gather(mem[:, j, :], mem_rows[j], list3[:, h * P // 16 : (h + 1) * P // 16], False)
+                gather(mem[:, j, :], mem_rows[j], list3[:, h * P // 16 : (h + 1) * P // 16], h == 0)
             o = bank(f"o{h}", [P, PACK, P], 2 + h)
             for j in range(PACK):
                 cols = slice(j * P, (j + 1) * P)

from contextlib import ExitStack

import concourse.mybir as mybir
from concourse.masks import make_identity

D, T, I, Q, E, G, M = 512, 2048, 512, 256, 512, 64, 1024
FLOPS = 2 * (2 * D * Q * T) + 2 * I * E * Q

F32 = mybir.dt.float32
BF16 = mybir.dt.bfloat16
I32 = mybir.dt.int32
U32 = mybir.dt.uint32
U16 = mybir.dt.uint16
U8 = mybir.dt.uint8
FP8X4 = mybir.dt.float8_e4m3fn_x4
FP4X4 = mybir.dt.float4_e2m1fn_x4
ALU = mybir.AluOpType
ACT = mybir.ActivationFunctionType
AXIS = mybir.AxisListType

P = 128
PACK = 4
BANK = 512
RUN = I // G
Q_TILES = Q // P


def tile_attend_planecos_outside_bymember_pl_kernel(
    tc, query, query2, keys_words, keys_scales, lam, slot_factor, vals, member, mgain, offs, offs2, offs3, out_0, out_1, out_2
):
    nc = tc.nc
    with ExitStack() as ctx:
        keep = ctx.enter_context(tc.tile_pool(name="keep", bufs=1))
        psum = ctx.enter_context(tc.psum_pool(name="psum", bufs=1))

        def sbuf(name, shape, dtype, tag=None):
            return keep.tile(shape, dtype, name=name, tag=tag or name, align_bytes=64)

        def bank(name, shape, tag):
            return psum.tile(shape, F32, name=name, tag=f"bank{tag}")

        q_raw = [sbuf(f"q_raw{n}", [P, PACK, Q], F32) for n in range(2)]
        k_words = [sbuf(f"k_words{n}", [P, T], U8) for n in range(2)]
        k_scales = sbuf("k_scales", [P, T], U8)
        list1 = keep.tile([P, I // 16], U16, name="list1")
        list2 = keep.tile([P, I // 16], U16, name="list2")
        list3 = keep.tile([P, Q // 16], U16, name="list3")
        lam_col = sbuf("lam_col", [P, Q_TILES], F32)
        os_rows = sbuf("os_rows", [P, I], F32)
        val_rows = [sbuf(f"val_rows{j}", [P, T], F32) for j in range(PACK)]
        mem_rows = [sbuf(f"mem_rows{j}", [P, M], F32) for j in range(PACK)]
        gain_rows = sbuf("gain_rows", [P, M], F32)

        nc.sync.dma_start(q_raw[0][:], query.rearrange("(p j) q -> p j q", j=PACK))
        for r in range(4):
            engine = nc.scalar if r else nc.sync
            engine.dma_start(k_scales[r:P:32, :].bitcast(I32), keys_scales[0, r:16:4, :].bitcast(I32))
        nc.sync.dma_start(k_words[0][:].bitcast(I32), keys_words[0, :, :T].bitcast(I32))
        nc.sync.dma_start(k_words[1][:].bitcast(I32), keys_words[0, :, T:].bitcast(I32))
        nc.sync.dma_start(q_raw[1][:], query2.rearrange("(p j) q -> p j q", j=PACK))
        nc.sync.dma_start(list3[:], offs3)
        nc.sync.dma_start(gain_rows[:], mgain)
        nc.sync.dma_start(list1[:], offs)
        nc.sync.dma_start(list2[:], offs2)
        with nc.allow_non_contiguous_dma(reason="one score factor a partition"):
            nc.sync.dma_start(lam_col[:], lam.rearrange("(h p) o -> p (h o)", p=P))
        vals_dealt = vals.rearrange("(p j) t -> p j t", j=PACK)
        for j in (0, 2, 1):
            nc.sync.dma_start(val_rows[j][:], vals_dealt[:, j, :])
        member_dealt = member.rearrange("(p j) m -> p j m", j=PACK)
        for j in range(PACK):
            nc.sync.dma_start(mem_rows[j][:], member_dealt[:, j, :])
        nc.sync.dma_start(val_rows[3][:], vals_dealt[:, 3, :])
        nc.sync.dma_start(os_rows[:], slot_factor[0].partition_broadcast(P))

        ident = sbuf("ident", [P, P], F32)
        make_identity(nc, ident[:])

        warm = sbuf("warm", [P, 1], F32)
        nc.scalar.activation(warm[:], ident[:, 0:1], ACT.Abs_reciprocal_sqrt, bias=0.5)

        q_words, q_scales = [], []
        for n in range(2):
            grouped = sbuf(f"q_grouped{n}", [P, Q, PACK], BF16)
            dst = grouped[:].rearrange("p (c i) t -> p c t i", i=4)
            src = q_raw[n][:].rearrange("p t (c i) -> p c t i", i=4)
            nc.vector.tensor_copy(dst, src)
            words = sbuf(f"q_words{n}", [P, Q], U32)
            scales = sbuf(f"q_scales{n}", [P, Q], U8)
            nc.vector.quantize_mx(words[:].bitcast(FP8X4), scales[:], grouped[:].rearrange("p q t -> p (q t)"))
            q_words.append(words)
            q_scales.append(scales)

        def scores(n, h, tag, on_vector):
            whole = sbuf(f"score{n}{h}", [P, T], F32)
            rows = slice(h * P, (h + 1) * P)
            for c in range(T // BANK):
                acc = bank(f"acc{n}{h}{c}", [P, BANK], tag + c)
                nc.tensor.matmul_mx(
                    acc[:],
                    lhsT=q_words[n][:, rows].bitcast(FP8X4),
                    lhsT_scale=q_scales[n][:, rows],
                    rhs=k_words[c // 2][:, 2 * BANK * (c % 2) : 2 * BANK * (c % 2 + 1)].bitcast(FP4X4),
                    rhs_scale=k_scales[:, BANK * c : BANK * (c + 1)],
                    start=True,
                    stop=True,
                )
                if c in on_vector:
                    nc.vector.tensor_copy(whole[:, BANK * c : BANK * (c + 1)], acc[:])
                else:
                    nc.scalar.activation(whole[:, BANK * c : BANK * (c + 1)], acc[:], ACT.Copy)
            return whole

        def gather(out, window, offsets, on_vector):
            if on_vector:
                nc.vector.tensor_copy(out, window[:].indirect(offsets))
            else:
                nc.scalar.activation(out, window[:].indirect(offsets), ACT.Copy)

        def look_up(name, window, offsets, on_vector, pieces=1, tag=None):
            picked = sbuf(name, [P, I], F32, tag=tag)
            width = I // pieces
            for n in range(pieces):
                gather(picked[:, n * width : (n + 1) * width], window, offsets[:, n * width // 16 : (n + 1) * width // 16], on_vector)
            return picked

        seen = {}

        def minus_ba(h, a2, b1):
            ba = sbuf(f"ba{h}", [P, I], F32)
            nc.vector.scalar_tensor_tensor(ba[:], b1[:], -1.0, a2[:], ALU.mult, ALU.mult)
            return ba

        def products(h, a1, a2, b1, b2, ba, engine, pieces):
            aa = sbuf(f"aa{h}", [P, I], F32)
            bb = sbuf(f"bb{h}", [P, I], F32)
            ab = sbuf(f"ab{h}", [P, I], F32)
            nc.gpsimd.tensor_tensor(aa[:], a1[:], a2[:], ALU.mult)
            width = I // pieces
            for n in range(pieces):
                cols = slice(n * width, (n + 1) * width)
                engine.tensor_tensor(bb[:, cols], b1[:, cols], b2[:, cols], ALU.mult)
                engine.tensor_tensor(ab[:, cols], a1[:, cols], b2[:, cols], ALU.mult)
            seen[h] = (aa, ba, bb, ab)
            sums = []
            for half in range(2):
                both = bank(f"both{h}{half}", [P, 2, 2, P], 2 * h + half)
                terms = [(0, aa), (1, ba), (0, bb), (1, ab)]
                for n, (which, term) in enumerate(terms):
                    for c in range(2):
                        cols = slice((2 * half + c) * P, (2 * half + c + 1) * P)
                        nc.tensor.matmul(
                            both[:, which, c, :],
                            term[:, cols],
                            ident[:],
                            start=(n == 0 and c == 0),
                            stop=(n == len(terms) - 1 and c == 1),
                            is_transpose=True,
                        )
                sums.append(both)
            return sums

        def inverse_root(name, both, engine):
            squares = sbuf(f"squares{name}", [P, 2, 2 * P], F32)
            nc.scalar.activation(squares[:], both[:].rearrange("s w c q -> s w (c q)"), ACT.Square)
            den = sbuf(f"den{name}", [P, 2 * P], F32)
            engine.tensor_tensor(den[:], squares[:, 0, :], squares[:, 1, :], ALU.add)
            inv = sbuf(f"inv{name}", [P, 2, P], F32)
            nc.scalar.activation(inv[:].rearrange("s c q -> s (c q)"), den[:], ACT.Abs_reciprocal_sqrt, bias=0.5)
            return inv

        a0 = scores(0, 0, 4, ())
        b0 = scores(1, 0, 0, ())
        gain = sbuf("gain", [P, Q], F32, tag="q_grouped1")
        gather(gain[:], gain_rows, list3[:], True)
        a01 = look_up("a01", a0, list1, True, tag="q_raw1")
        a02 = look_up("a02", a0, list2, True)
        a1 = scores(0, 1, 0, ())
        b01 = look_up("b01", b0, list1, True)
        ba0 = minus_ba(0, a02, b01)
        b02 = look_up("b02", b0, list2, True)
        b1 = scores(1, 1, 0, ())
        sums = [products(0, a01, a02, b01, b02, ba0, nc.gpsimd, 1)]
        a11 = look_up("a11", a1, list1, True)
        a12 = look_up("a12", a1, list2, True)
        b11 = look_up("b11", b1, list1, True)
        b12 = look_up("b12", b1, list2, False, 2)
        sums.append(products(1, a11, a12, b11, b12, minus_ba(1, a12, b11), nc.vector, 2))
        invs = [[inverse_root(f"{h}{half}", sums[h][half], (nc.gpsimd, nc.vector)[h]) for half in range(2)] for h in range(Q_TILES)]

        cos_banks = []
        for h in range(Q_TILES):
            cos = bank(f"cos{h}", [P, PACK, P], 5 + h)
            for half in range(2):
                cos_t = sbuf(f"cos_t{h}{half}", [P, 2, P], F32)
                nc.vector.tensor_tensor(cos_t[:], sums[h][half][:, 0, :, :], invs[h][half][:], ALU.mult)
                for c in range(2):
                    nc.tensor.transpose(cos[:, 2 * half + c, :], cos_t[:, c, :], ident[:])
            cos_banks.append(cos)

        ps, zs = [], []
        for h in range(Q_TILES):
            p = sbuf(f"p{h}", [P, I], F32, tag=f"den1{1 - h}")
            z0 = sbuf(f"z0{h}", [P, 1], F32)
            nc.scalar.activation(
                p[:], cos_banks[h][:].rearrange("q c s -> q (c s)"), ACT.Exp, scale=lam_col[:, h : h + 1], accum_out=z0[:]
            )
            ps.append(p)
            zs.append(z0)

        def values(half, on_vector, tags):
            turned = bank(f"v_turned{half}", [P, 2, 2, P], half)
            for jj in range(2):
                j = 2 * half + jj
                picked = sbuf(f"v_picked{j}", [P, I], BF16, tag=tags[jj])
                gather(picked[:], val_rows[j], list1[:], on_vector[jj])
                pairs = picked[:].bitcast(F32)
                for u in range(2):
                    nc.tensor.transpose(turned[:, jj, u, :], pairs[:, u : I // 2 : 2], ident[:])
            grouped = sbuf(f"v_grouped{half}", [P, 2 * P * PACK], BF16)
            nc.scalar.copy(
                grouped[:].bitcast(F32).rearrange("s (j e u) -> s j e u", j=2, u=2), turned[:].rearrange("s j u e -> s j e u")
            )
            return grouped

        v_grouped = [values(0, (False, True), ("b01", "inv11")), values(1, (True, False), ("b12", "cos_t11"))]

        tiles = range(Q_TILES)
        pg = [sbuf(f"pg{h}", [P, G], F32) for h in tiles]
        rest = [sbuf(f"rest{h}", [P, G], F32) for h in tiles]
        k0 = [sbuf(f"k0{h}", [P, G], F32) for h in tiles]
        for h in tiles:
            nc.vector.tensor_reduce(pg[h][:], ps[h][:].rearrange("q (g e) -> q g e", e=RUN), AXIS.X, ALU.add)
        for h in tiles:
            nc.vector.tensor_scalar(rest[h][:], pg[h][:], -1.0, zs[h][:], ALU.mult, ALU.add)
        for h in tiles:
            nc.vector.reciprocal(k0[h][:], rest[h][:])
        w_grouped = []
        for h in tiles:
            p_os = sbuf(f"p_os{h}", [P, I], F32, tag=("p_os0", "pg1")[h])
            nc.gpsimd.tensor_tensor(p_os[:], ps[h][:], os_rows[:], ALU.mult)
            w = sbuf(f"w{h}", [P, I], BF16)
            nc.vector.tensor_tensor(
                w[:].rearrange("q (g e) -> q g e", e=RUN),
                p_os[:].rearrange("q (g e) -> q g e", e=RUN),
                k0[h][:].unsqueeze(2).to_broadcast([P, G, RUN]),
                ALU.mult,
            )
            w_turned = bank(f"w_turned{h}", [P, 2, P], 5 + h)
            pairs = w[:].bitcast(F32)
            for u in range(2):
                nc.tensor.transpose(w_turned[:, u, :], pairs[:, u : I // 2 : 2], ident[:])
            grouped = sbuf(f"w_grouped{h}", [P, P * PACK], BF16)
            nc.scalar.copy(grouped[:].bitcast(F32).rearrange("s (q u) -> s q u", u=2), w_turned[:].rearrange("s u q -> s q u"))
            w_grouped.append(grouped)

        v_words = sbuf("v_words", [P, E], U32, tag="pg1")
        v_scales = sbuf("v_scales", [P, E], U8)
        for half in range(2):
            cols = slice(2 * P * half, 2 * P * (half + 1))
            nc.vector.quantize_mx(v_words[:, cols].bitcast(FP8X4), v_scales[:, cols], v_grouped[half][:])
        w_quantised = []
        for h in tiles:
            w_words = sbuf(f"w_words{h}", [P, P], U32)
            w_scales = sbuf(f"w_scales{h}", [P, P], U8)
            nc.vector.quantize_mx(w_words[:].bitcast(FP8X4), w_scales[:], w_grouped[h][:])
            w_quantised.append((w_words, w_scales))

        y_words = sbuf("y_words", [P, Q], U32)
        y_scales = sbuf("y_scales", [P, Q], U8)
        out_dealt = out_0.rearrange("(p j) q -> p j q", j=PACK)
        for h in range(Q_TILES):
            w_words, w_scales = w_quantised[h]
            mem = sbuf(f"mem{h}", [P, PACK, P], F32, tag=("inv10", "w1")[h])
            for j in range(PACK):
                gather(mem[:, j, :], mem_rows[j], list3[:, h * P // 16 : (h + 1) * P // 16], h == 0)
            o = bank(f"o{h}", [P, PACK, P], 2 + h)
            for j in range(PACK):
                cols = slice(j * P, (j + 1) * P)
                nc.tensor.matmul_mx(
                    o[:, j, :],
                    lhsT=v_words[:, cols].bitcast(FP8X4),
                    lhsT_scale=v_scales[:, cols],
                    rhs=w_words[:].bitcast(FP8X4),
                    rhs_scale=w_scales[:],
                    start=True,
                    stop=True,
                )
            scaled = sbuf(f"scaled{h}", [P, PACK, P], F32)
            y = sbuf(f"y{h}", [P, PACK, P], F32)
            y_grouped = sbuf(f"y_grouped{h}", [P, P, PACK], BF16)
            width = P // (h + 1)
            pieces = [slice(start, start + width) for start in range(0, P, width)]
            for cols in pieces:
                rows = slice(h * P + cols.start, h * P + cols.stop)
                nc.vector.tensor_tensor(
                    scaled[:, :, cols], o[:, :, cols], gain[:, rows].unsqueeze(1).to_broadcast([P, PACK, width]), ALU.mult
                )
            for cols in pieces:
                rows = slice(h * P + cols.start, h * P + cols.stop)
                nc.vector.tensor_tensor(y[:, :, cols], scaled[:, :, cols], mem[:, :, cols], ALU.add)
                nc.scalar.copy(y_grouped[:, cols, :], y[:, :, cols].rearrange("p j q -> p q j"))
            for cols in pieces:
                rows = slice(h * P + cols.start, h * P + cols.stop)
                nc.vector.quantize_mx(
                    y_words[:, rows].bitcast(FP8X4), y_scales[:, rows], y_grouped[:, cols, :].rearrange("p q j -> p (q j)")
                )
            nc.sync.dma_start(out_dealt[:, :, h * P : (h + 1) * P], y[:])

        nc.sync.dma_start(out_1[0].rearrange("p q j -> p (q j)").bitcast(I32), y_words[:].bitcast(I32))
        for r in range(4):
            engine = nc.scalar if r % 2 else nc.sync
            engine.dma_start(out_2[0, r:16:4, :].bitcast(I32), y_scales[r:P:32, :].bitcast(I32))
